import numpy as np
import ml_dtypes


def mxq(x, axis, fmt="e4m3"):
    dtype, down = {"e4m3": (ml_dtypes.float8_e4m3fn, 7), "e5m2": (ml_dtypes.float8_e5m2, 14)}[fmt]
    v = np.moveaxis(np.asarray(x, np.float32).astype(ml_dtypes.bfloat16).astype(np.float64), axis, -1)
    blocks = v.reshape(v.shape[:-1] + (-1, 32))
    amax = np.abs(blocks).max(-1, keepdims=True)
    byte = np.maximum(np.where(amax > 0, np.frexp(amax)[1] - 1 + 127, 0) - down, 1)
    scale = np.exp2(byte - 127.0)
    codes = (blocks / scale).astype(np.float32).astype(dtype).astype(np.float64)
    return np.moveaxis((codes * scale).reshape(v.shape), -1, axis)


WIDE = False


def mx_kscale(k):
    if not WIDE:
        return np.ones(k)
    levels = np.array([10, -10, 5, -5, 0])
    if k % 512:
        return np.exp2(np.random.permutation(np.resize(levels, k // 32))).repeat(32)
    a = np.empty((k // 512, 16))
    for p in range(k // 512):
        a[p, :8] = np.random.permutation(np.resize(levels, 8))
        for g in range(8):
            far = levels[np.abs(levels - a[p, g]) >= 10]
            a[p, g + 8] = far[np.random.randint(len(far))]
    return np.exp2(a.ravel()).repeat(32)


def f64(x):
    return np.asarray(x).astype(np.float64)


def striped(idx):
    return np.tile(idx.reshape(-1, 16).T, (8, 1)).astype(np.uint16)


def unstriped(offs):
    return offs[:16].T.reshape(-1).astype(np.int64)


def relu(v):
    return np.maximum(v, 0.0)


K, T, S, V, H, N = 1024, 1024, 512, 256, 512, 256


def setup_inputs():
    n = np.random.standard_normal
    s = mx_kscale(K)[:, None]
    u = mx_kscale(H)
    return {
        "xT": (n((K, T)) * s).astype(np.float32),
        "w1": (n((K, H)) / np.sqrt(K) / s * u).astype(np.float32),
        "w2": (n((H, N)) / np.sqrt(2 * H) / u[:, None]).astype(np.float32),
        "w3": (n((H, N)) / np.sqrt(2 * H) / u[:, None]).astype(np.float32),
        "offs": striped(np.random.permutation(T)[:S]),
        "cen": striped(np.random.permutation(S)[:V]),
        "pos1": striped(np.random.permutation(S)[:V]),
        "pos2": striped(np.random.permutation(S)[:V]),
    }


def reference(xT, w1, w2, w3, offs, cen, pos1, pos2):
    xq = mxq(f64(xT)[:, unstriped(offs)], 0, "e4m3")
    h = relu(mxq(f64(w1), 0, "e4m3").T @ xq)
    hc = h[:, unstriped(cen)]
    z = np.maximum(h[:, unstriped(pos1)], h[:, unstriped(pos2)])
    return relu(mxq(f64(w2), 0, "e4m3").T @ mxq(hc, 0, "e4m3") + mxq(f64(w3), 0, "e4m3").T @ mxq(z, 0, "e4m3"))

@@ -1,0 +1,201 @@
+from contextlib import ExitStack
+
+import concourse.mybir as mybir
+
+K, T, S, V, H, N = 1024, 1024, 512, 256, 512, 256
+FLOPS = 2 * K * H * S + 2 * 2 * H * N * V
+
+F32 = mybir.dt.float32
+BF16 = mybir.dt.bfloat16
+U32 = mybir.dt.uint32
+U16 = mybir.dt.uint16
+U8 = mybir.dt.uint8
+FP8X4 = mybir.dt.float8_e4m3fn_x4
+COPY = mybir.ActivationFunctionType.Copy
+RELU = mybir.ActivationFunctionType.Relu
+MAX = mybir.AluOpType.max
+
+P = 128
+PACK = 4
+K_PASS = P * PACK
+PASSES = K // K_PASS
+X_CHUNK = 256
+W_CHUNKS = ((256, 256), (256, 128, 128))
+W_VECTOR = ((0, 0), (32, 16, 20))
+HALF = V // 2
+
+
+def tile_picked_sagecat_maxrelu_e_kernel(tc, xT, w1, w2, w3, offs, cen, pos1, pos2, out):
+    nc = tc.nc
+    with ExitStack() as ctx:
+        keep = ctx.enter_context(tc.tile_pool(name="keep", bufs=1))
+        psum = ctx.enter_context(tc.psum_pool(name="psum", bufs=1))
+
+        def load_list(src, name):
+            tile = keep.tile(list(src.shape), U16, name=name)
+            nc.sync.dma_start(tile[:], src)
+            return tile
+
+        def load_rows(src, z, c0, width, name):
+            raw = keep.tile([P, PACK, width], F32, name=name, tag=name, align_bytes=64)
+            rows = src[z * K_PASS : (z + 1) * K_PASS, c0 : c0 + width]
+            nc.sync.dma_start(out=raw[:], in_=rows.rearrange("(p j) w -> p j w", j=PACK))
+            return raw
+
+        def interleave(engine, grouped, planes):
+            dst = grouped.rearrange("p (c i) j -> p c j i", i=4)
+            src = planes.rearrange("p j (c i) -> p c j i", i=4)
+            if engine == "vector":
+                nc.vector.tensor_copy(out=dst, in_=src)
+            else:
+                nc.scalar.activation(out=dst, in_=src, func=COPY)
+
+        def quantize(codes, scales, grouped):
+            nc.vector.quantize_mx(out=codes.bitcast(FP8X4), scales=scales, in_=grouped)
+
+        x_chunks = T // X_CHUNK
+        x_raw = {}
+        for z in range(PASSES):
+            for c in range(x_chunks):
+                x_raw[z, c] = load_rows(xT, z, c * X_CHUNK, X_CHUNK, "x_raw%d_%d" % (z, c))
+                if z == 0 and c == 0:
+                    offs_sb = load_list(offs, "offs_sb")
+        w1_raw = {}
+        for z in range(PASSES):
+            for c, width in enumerate(W_CHUNKS[z]):
+                w1_raw[z, c] = load_rows(w1, z, sum(W_CHUNKS[z][:c]), width, "w1_raw%d_%d" % (z, c))
+        pos1_sb = load_list(pos1, "pos1_sb")
+        pos2_sb = load_list(pos2, "pos2_sb")
+        cen_sb = load_list(cen, "cen_sb")
+        w3_raw = load_rows(w3, 0, 0, N, "w3_raw")
+        w2_raw = load_rows(w2, 0, 0, N, "w2_raw")
+
+        x_scales = keep.tile([P, T], U8, name="x_scales", align_bytes=64)
+        nc.gpsimd.memset(x_scales[:], 0)
+        picked_words = []
+        for z in range(PASSES):
+            x_words = keep.tile([P, T], U32, name="x_words%d" % z, align_bytes=64)
+            for c in range(x_chunks):
+                x_bf = keep.tile([P, X_CHUNK, PACK], BF16, name="x_bf%d_%d" % (z, c), align_bytes=64)
+                raw = x_raw[z, c]
+                if z == PASSES - 1 and c == x_chunks - 1:
+                    cut = 160
+                    interleave("vector", x_bf[:, :cut, :], raw[:, :, :cut])
+                    interleave("scalar", x_bf[:, cut:, :], raw[:, :, cut:])
+                else:
+                    interleave("scalar" if c % 2 == 0 else "vector", x_bf[:], raw[:])
+                cols = slice(c * X_CHUNK, (c + 1) * X_CHUNK)
+                quantize(x_words[:, cols], x_scales[4 * z :, cols], x_bf[:].rearrange("p c j -> p (c j)"))
+            picked = keep.tile([P, S], U32, name="picked_words%d" % z, align_bytes=64)
+            nc.vector.tensor_copy(out=picked[:], in_=x_words[:].indirect(offs_sb[:]))
+            picked_words.append(picked)
+        picked_scales = keep.tile([P, S], U8, name="picked_scales", align_bytes=64)
+        nc.vector.tensor_copy(out=picked_scales[:], in_=x_scales[:].indirect(offs_sb[:]))
+
+        def deal(engine, w_bf, raw, m0, lo, hi):
+            dst = w_bf[:, :, m0 + lo : m0 + hi, :].rearrange("p t (a b) j -> p a j b t", b=2)
+            src = raw[:, :, PACK * lo : PACK * hi].rearrange("p j (a b t) -> p a j b t", b=2, t=PACK)
+            if engine == "vector":
+                nc.vector.tensor_copy(out=dst, in_=src)
+            else:
+                nc.scalar.copy(out=dst, in_=src)
+
+        w1_words, w1_scales = [], []
+        for z in range(PASSES):
+            w_bf = keep.tile([P, PACK, P, PACK], BF16, name="w1_bf%d" % z, align_bytes=64)
+            for c, width in enumerate(W_CHUNKS[z]):
+                m0, cut = sum(W_CHUNKS[z][:c]) // PACK, W_VECTOR[z][c]
+                if cut:
+                    deal("vector", w_bf, w1_raw[z, c], m0, 0, cut)
+                deal("scalar", w_bf, w1_raw[z, c], m0, cut, width // PACK)
+            words = keep.tile([P, H], U32, name="w1_words%d" % z, align_bytes=64)
+            scales = keep.tile([P, H], U8, name="w1_scales%d" % z, align_bytes=64)
+            if z == 0:
+                quantize(words[:], scales[:], w_bf[:].rearrange("p t m j -> p (t m j)"))
+            else:
+                for t in range(PACK):
+                    cols = slice(t * P, (t + 1) * P)
+                    quantize(words[:, cols], scales[:, cols], w_bf[:, t, :, :].rearrange("p m j -> p (m j)"))
+            w1_words.append(words)
+            w1_scales.append(scales)
+
+        h = []
+        for t in range(PACK):
+            cols = slice(t * P, (t + 1) * P)
+            h_t = keep.tile([P, S], F32, name="h%d" % t)
+            width = S // 2 if t == 0 else S
+            accs = [psum.tile([P, width], F32, name="acc%d_%d" % (t, b), tag="acc%d_%d" % (t, b)) for b in range(S // width)]
+            for z in range(PASSES):
+                for b, acc in enumerate(accs):
+                    nodes = slice(b * width, (b + 1) * width)
+                    nc.tensor.matmul_mx(
+                        out=acc[:],
+                        lhsT=w1_words[z][:, cols].bitcast(FP8X4),
+                        lhsT_scale=w1_scales[z][:, cols],
+                        rhs=picked_words[z][:, nodes].bitcast(FP8X4),
+                        rhs_scale=picked_scales[4 * z :, nodes],
+                        start=(z == 0),
+                        stop=(z == PASSES - 1),
+                    )
+            for b, acc in enumerate(accs):
+                nc.scalar.activation(out=h_t[:, b * width : (b + 1) * width], in_=acc[:], func=RELU)
+            h.append(h_t)
+
+        first = keep.tile([P, PACK, V], BF16, name="first", tag="planes")
+        second = keep.tile([P, PACK, V], BF16, name="second")
+        for t in range(PACK):
+            nc.vector.tensor_copy(out=first[:, t, :], in_=h[t][:].indirect(pos1_sb[:]))
+            nc.vector.tensor_copy(out=second[:, t, :], in_=h[t][:].indirect(pos2_sb[:]))
+
+        w23_bf = keep.tile([P, 2 * N, PACK], BF16, name="w23_bf", tag="w23_bf", align_bytes=64)
+        interleave("scalar", w23_bf[:, :N, :], w3_raw[:])
+        interleave("scalar", w23_bf[:, N:, :], w2_raw[:])
+        w23_words = keep.tile([P, 2 * N], U32, name="w23_words", align_bytes=64)
+        w23_scales = keep.tile([P, 2 * N], U8, name="w23_scales", align_bytes=64)
+        quantize(w23_words[:], w23_scales[:], w23_bf[:].rearrange("p c j -> p (c j)"))
+
+        largest = keep.tile([P, PACK, V], BF16, name="largest")
+        nc.vector.tensor_tensor(out=largest[:], in0=first[:], in1=second[:], op=MAX)
+        z_bf = keep.tile([P, V, PACK], BF16, name="z_bf", tag="w2_raw", align_bytes=64)
+        interleave("scalar", z_bf[:], largest[:])
+        z_words = keep.tile([P, V], U32, name="z_words", align_bytes=64)
+        z_scales = keep.tile([P, V], U8, name="z_scales", align_bytes=64)
+
+        centre = []
+        for half in range(2):
+            if half == 0:
+                planes = keep.tile([P, PACK, HALF], BF16, name="centre0", tag="planes")
+            else:
+                planes = keep.tile([P, PACK, HALF], BF16, name="centre1", tag="w23_bf", align_bytes=64)
+            entries = cen_sb[:, half * HALF // 16 : (half + 1) * HALF // 16]
+            for t in range(PACK):
+                nc.vector.tensor_copy(out=planes[:, t, :], in_=h[t][:].indirect(entries))
+            centre.append(planes)
+        quantize(z_words[:], z_scales[:], z_bf[:].rearrange("p c j -> p (c j)"))
+
+        for half in range(2):
+            targets = slice(half * HALF, (half + 1) * HALF)
+            if half == 0:
+                c_bf = keep.tile([P, HALF, PACK], BF16, name="c_bf0", align_bytes=64)
+                interleave("scalar", c_bf[:], centre[half][:])
+            else:
+                c_bf = keep.tile([P, HALF, PACK], BF16, name="c_bf1", tag="w2_raw", align_bytes=64)
+                interleave("vector", c_bf[:], centre[half][:])
+            c_words = keep.tile([P, HALF], U32, name="c_words%d" % half, align_bytes=64)
+            c_scales = keep.tile([P, HALF], U8, name="c_scales%d" % half, align_bytes=64)
+            quantize(c_words[:], c_scales[:], c_bf[:].rearrange("p c j -> p (c j)"))
+
+            staged = keep.tile([P, N // P, HALF], F32, name="staged%d" % half)
+            for a in range(N // P):
+                res = psum.tile([P, HALF], F32, name="res%d_%d" % (half, a), tag="acc%d_0" % (2 * half + a))
+                c3 = slice(a * P, (a + 1) * P)
+                c2 = slice(N + a * P, N + (a + 1) * P)
+                nc.tensor.matmul_mx(out=res[:], lhsT=w23_words[:, c3].bitcast(FP8X4), lhsT_scale=w23_scales[:, c3],
+                                    rhs=z_words[:, targets].bitcast(FP8X4), rhs_scale=z_scales[:, targets], start=True, stop=False)
+                nc.tensor.matmul_mx(out=res[:], lhsT=w23_words[:, c2].bitcast(FP8X4), lhsT_scale=w23_scales[:, c2],
+                                    rhs=c_words[:].bitcast(FP8X4), rhs_scale=c_scales[:], start=False, stop=True)
+                if half == 0 or a == 0:
+                    nc.scalar.activation(out=staged[:, a, :], in_=res[:], func=RELU)
+                else:
+                    nc.vector.tensor_scalar(out=staged[:, a, :], in0=res[:], scalar1=0.0, scalar2=None, op0=MAX)
+            nc.sync.dma_start(out=out[:, targets].rearrange("(a p) v -> p a v", p=P), in_=staged[:])

@@ -19,9 +19,10 @@ P = 128
 PACK = 4
 K_PASS = P * PACK
 PASSES = K // K_PASS
-X_CHUNK = 256
-W_CHUNKS = ((256, 256), (256, 128, 128))
-W_VECTOR = ((0, 0), (32, 16, 20))
+X_CHUNKS = ((512, 512), (512, 256, 256))
+X_VECTOR = ((256, 256), (192, 256, 112))
+W_CHUNKS = ((256, 256), (256, 256))
+W_VECTOR = ((0, 0), (28, 40))
 HALF = V // 2
 
 
@@ -53,11 +54,10 @@ def tile_picked_sagecat_maxrelu_e_kernel(tc, xT, w1, w2, w3, offs, cen, pos1, po
         def quantize(codes, scales, grouped):
             nc.vector.quantize_mx(out=codes.bitcast(FP8X4), scales=scales, in_=grouped)
 
-        x_chunks = T // X_CHUNK
         x_raw = {}
         for z in range(PASSES):
-            for c in range(x_chunks):
-                x_raw[z, c] = load_rows(xT, z, c * X_CHUNK, X_CHUNK, "x_raw%d_%d" % (z, c))
+            for c, width in enumerate(X_CHUNKS[z]):
+                x_raw[z, c] = load_rows(xT, z, sum(X_CHUNKS[z][:c]), width, "x_raw%d_%d" % (z, c))
                 if z == 0 and c == 0:
                     offs_sb = load_list(offs, "offs_sb")
         w1_raw = {}
@@ -75,16 +75,13 @@ def tile_picked_sagecat_maxrelu_e_kernel(tc, xT, w1, w2, w3, offs, cen, pos1, po
         picked_words = []
         for z in range(PASSES):
             x_words = keep.tile([P, T], U32, name="x_words%d" % z, align_bytes=64)
-            for c in range(x_chunks):
-                x_bf = keep.tile([P, X_CHUNK, PACK], BF16, name="x_bf%d_%d" % (z, c), align_bytes=64)
-                raw = x_raw[z, c]
-                if z == PASSES - 1 and c == x_chunks - 1:
-                    cut = 160
-                    interleave("vector", x_bf[:, :cut, :], raw[:, :, :cut])
+            for c, width in enumerate(X_CHUNKS[z]):
+                x_bf = keep.tile([P, width, PACK], BF16, name="x_bf%d_%d" % (z, c), align_bytes=64)
+                raw, cut, c0 = x_raw[z, c], X_VECTOR[z][c], sum(X_CHUNKS[z][:c])
+                interleave("vector", x_bf[:, :cut, :], raw[:, :, :cut])
+                if cut < width:
                     interleave("scalar", x_bf[:, cut:, :], raw[:, :, cut:])
-                else:
-                    interleave("scalar" if c % 2 == 0 else "vector", x_bf[:], raw[:])
-                cols = slice(c * X_CHUNK, (c + 1) * X_CHUNK)
+                cols = slice(c0, c0 + width)
                 quantize(x_words[:, cols], x_scales[4 * z :, cols], x_bf[:].rearrange("p c j -> p (c j)"))
             picked = keep.tile([P, S], U32, name="picked_words%d" % z, align_bytes=64)
             nc.vector.tensor_copy(out=picked[:], in_=x_words[:].indirect(offs_sb[:]))
@@ -100,24 +97,30 @@ def tile_picked_sagecat_maxrelu_e_kernel(tc, xT, w1, w2, w3, offs, cen, pos1, po
             else:
                 nc.scalar.copy(out=dst, in_=src)
 
-        w1_words, w1_scales = [], []
+        w1_bf, w1_scales = [], []
         for z in range(PASSES):
             w_bf = keep.tile([P, PACK, P, PACK], BF16, name="w1_bf%d" % z, align_bytes=64)
             for c, width in enumerate(W_CHUNKS[z]):
                 m0, cut = sum(W_CHUNKS[z][:c]) // PACK, W_VECTOR[z][c]
                 if cut:
                     deal("vector", w_bf, w1_raw[z, c], m0, 0, cut)
-                deal("scalar", w_bf, w1_raw[z, c], m0, cut, width // PACK)
-            words = keep.tile([P, H], U32, name="w1_words%d" % z, align_bytes=64)
+                if cut < width // PACK:
+                    deal("scalar", w_bf, w1_raw[z, c], m0, cut, width // PACK)
+            w1_bf.append(w_bf)
             scales = keep.tile([P, H], U8, name="w1_scales%d" % z, align_bytes=64)
-            if z == 0:
-                quantize(words[:], scales[:], w_bf[:].rearrange("p t m j -> p (t m j)"))
-            else:
-                for t in range(PACK):
-                    cols = slice(t * P, (t + 1) * P)
-                    quantize(words[:, cols], scales[:, cols], w_bf[:, t, :, :].rearrange("p m j -> p (m j)"))
-            w1_words.append(words)
             w1_scales.append(scales)
+        head0 = keep.tile([P, P], U32, name="w1_words0_head", align_bytes=64)
+        rest0 = keep.tile([P, H - P], U32, name="w1_words0_rest", tag="w1_raw1_1", align_bytes=64)
+        words1 = keep.tile([P, H], U32, name="w1_words1", tag="w23_bf", align_bytes=64)
+
+        def w1_words(z, t0, t1):
+            if z == 1:
+                return words1[:, t0 * P : t1 * P]
+            return head0[:] if t0 == 0 else rest0[:, (t0 - 1) * P : (t1 - 1) * P]
+
+        for t0, t1 in ((0, 1), (1, 2), (2, 4)):
+            for z in range(PASSES):
+                quantize(w1_words(z, t0, t1), w1_scales[z][:, t0 * P : t1 * P], w1_bf[z][:, t0:t1, :, :].rearrange("p t m j -> p (t m j)"))
 
         h = []
         for t in range(PACK):
@@ -130,7 +133,7 @@ def tile_picked_sagecat_maxrelu_e_kernel(tc, xT, w1, w2, w3, offs, cen, pos1, po
                     nodes = slice(b * width, (b + 1) * width)
                     nc.tensor.matmul_mx(
                         out=acc[:],
-                        lhsT=w1_words[z][:, cols].bitcast(FP8X4),
+                        lhsT=w1_words(z, t, t + 1).bitcast(FP8X4),
                         lhsT_scale=w1_scales[z][:, cols],
                         rhs=picked_words[z][:, nodes].bitcast(FP8X4),
                         rhs_scale=picked_scales[4 * z :, nodes],

@@ -19,11 +19,14 @@ P = 128
 PACK = 4
 K_PASS = P * PACK
 PASSES = K // K_PASS
-X_CHUNKS = ((512, 512), (512, 256, 256))
-X_VECTOR = ((256, 256), (192, 256, 112))
-W_CHUNKS = ((256, 256), (256, 256))
-W_VECTOR = ((0, 0), (28, 40))
+SCALE_ROWS = 4
+LIST_ROWS = 16
 HALF = V // 2
+
+X_LOADS = (((512, 256), (512, 320)), ((256, 0), (256, 0), (256, 128), (128, 0), (128, 128)))
+W_LOADS = (((256, 0), (256, 0)), ((256, 128), (128, 128)))
+W_LAST = 128
+EARLY_TILES = 2
 
 
 def tile_picked_sagecat_maxrelu_e_kernel(tc, xT, w1, w2, w3, offs, cen, pos1, pos2, out):
@@ -51,19 +54,34 @@ def tile_picked_sagecat_maxrelu_e_kernel(tc, xT, w1, w2, w3, offs, cen, pos1, po
             else:
                 nc.scalar.activation(out=dst, in_=src, func=COPY)
 
-        def quantize(codes, scales, grouped):
-            nc.vector.quantize_mx(out=codes.bitcast(FP8X4), scales=scales, in_=grouped)
+        def quantize(words, scales, grouped):
+            nc.vector.quantize_mx(out=words.bitcast(FP8X4), scales=scales, in_=grouped)
+
+        def multiply(acc, lhs_words, lhs_scales, rhs_words, rhs_scales, start, stop):
+            nc.tensor.matmul_mx(
+                out=acc,
+                lhsT=lhs_words.bitcast(FP8X4),
+                lhsT_scale=lhs_scales,
+                rhs=rhs_words.bitcast(FP8X4),
+                rhs_scale=rhs_scales,
+                start=start,
+                stop=stop,
+            )
+
+        def starts(loads):
+            return [sum(width for width, share in loads[:c]) for c in range(len(loads))]
 
         x_raw = {}
         for z in range(PASSES):
-            for c, width in enumerate(X_CHUNKS[z]):
-                x_raw[z, c] = load_rows(xT, z, sum(X_CHUNKS[z][:c]), width, "x_raw%d_%d" % (z, c))
-                if z == 0 and c == 0:
+            for c, c0 in enumerate(starts(X_LOADS[z])):
+                x_raw[z, c] = load_rows(xT, z, c0, X_LOADS[z][c][0], "x_raw%d_%d" % (z, c))
+                if (z, c) == (0, 0):
                     offs_sb = load_list(offs, "offs_sb")
         w1_raw = {}
         for z in range(PASSES):
-            for c, width in enumerate(W_CHUNKS[z]):
-                w1_raw[z, c] = load_rows(w1, z, sum(W_CHUNKS[z][:c]), width, "w1_raw%d_%d" % (z, c))
+            for c, c0 in enumerate(starts(W_LOADS[z])):
+                w1_raw[z, c] = load_rows(w1, z, c0, W_LOADS[z][c][0], "w1_raw%d_%d" % (z, c))
+        w1_last = load_rows(w1, PASSES - 1, H - W_LAST, W_LAST, "w1_last")
         pos1_sb = load_list(pos1, "pos1_sb")
         pos2_sb = load_list(pos2, "pos2_sb")
         cen_sb = load_list(cen, "cen_sb")
@@ -75,130 +93,140 @@ def tile_picked_sagecat_maxrelu_e_kernel(tc, xT, w1, w2, w3, offs, cen, pos1, po
         picked_words = []
         for z in range(PASSES):
             x_words = keep.tile([P, T], U32, name="x_words%d" % z, align_bytes=64)
-            for c, width in enumerate(X_CHUNKS[z]):
-                x_bf = keep.tile([P, width, PACK], BF16, name="x_bf%d_%d" % (z, c), align_bytes=64)
-                raw, cut, c0 = x_raw[z, c], X_VECTOR[z][c], sum(X_CHUNKS[z][:c])
-                interleave("vector", x_bf[:, :cut, :], raw[:, :, :cut])
-                if cut < width:
-                    interleave("scalar", x_bf[:, cut:, :], raw[:, :, cut:])
-                cols = slice(c0, c0 + width)
-                quantize(x_words[:, cols], x_scales[4 * z :, cols], x_bf[:].rearrange("p c j -> p (c j)"))
+            for c, c0 in enumerate(starts(X_LOADS[z])):
+                width, share = X_LOADS[z][c]
+                x_grouped = keep.tile([P, width, PACK], BF16, name="x_grouped%d_%d" % (z, c), align_bytes=64)
+                if share > 0:
+                    interleave("vector", x_grouped[:, :share, :], x_raw[z, c][:, :, :share])
+                if share < width:
+                    interleave("scalar", x_grouped[:, share:, :], x_raw[z, c][:, :, share:])
+                nodes = slice(c0, c0 + width)
+                quantize(x_words[:, nodes], x_scales[SCALE_ROWS * z :, nodes], x_grouped[:].rearrange("p c j -> p (c j)"))
             picked = keep.tile([P, S], U32, name="picked_words%d" % z, align_bytes=64)
             nc.vector.tensor_copy(out=picked[:], in_=x_words[:].indirect(offs_sb[:]))
             picked_words.append(picked)
         picked_scales = keep.tile([P, S], U8, name="picked_scales", align_bytes=64)
         nc.vector.tensor_copy(out=picked_scales[:], in_=x_scales[:].indirect(offs_sb[:]))
 
-        def deal(engine, w_bf, raw, m0, lo, hi):
-            dst = w_bf[:, :, m0 + lo : m0 + hi, :].rearrange("p t (a b) j -> p a j b t", b=2)
-            src = raw[:, :, PACK * lo : PACK * hi].rearrange("p j (a b t) -> p a j b t", b=2, t=PACK)
-            if engine == "vector":
-                nc.vector.tensor_copy(out=dst, in_=src)
-            else:
-                nc.scalar.copy(out=dst, in_=src)
+        def dealt_views(grouped, raw, c0, lo, hi):
+            places = slice((c0 + lo) // PACK, (c0 + hi) // PACK)
+            dst = grouped[:, :, places, :].rearrange("p t (a b) j -> p a j b t", b=2)
+            src = raw[:, :, lo:hi].rearrange("p j (a b t) -> p a j b t", b=2, t=PACK)
+            return dst, src
 
-        w1_bf, w1_scales = [], []
+        w1_grouped, w1_scales = [], []
         for z in range(PASSES):
-            w_bf = keep.tile([P, PACK, P, PACK], BF16, name="w1_bf%d" % z, align_bytes=64)
-            for c, width in enumerate(W_CHUNKS[z]):
-                m0, cut = sum(W_CHUNKS[z][:c]) // PACK, W_VECTOR[z][c]
-                if cut:
-                    deal("vector", w_bf, w1_raw[z, c], m0, 0, cut)
-                if cut < width // PACK:
-                    deal("scalar", w_bf, w1_raw[z, c], m0, cut, width // PACK)
-            w1_bf.append(w_bf)
-            scales = keep.tile([P, H], U8, name="w1_scales%d" % z, align_bytes=64)
-            w1_scales.append(scales)
-        head0 = keep.tile([P, P], U32, name="w1_words0_head", align_bytes=64)
-        rest0 = keep.tile([P, H - P], U32, name="w1_words0_rest", tag="w1_raw1_1", align_bytes=64)
-        words1 = keep.tile([P, H], U32, name="w1_words1", tag="w23_bf", align_bytes=64)
+            grouped = keep.tile([P, PACK, P, PACK], BF16, name="w1_grouped%d" % z, align_bytes=64)
+            for c, c0 in enumerate(starts(W_LOADS[z])):
+                width, share = W_LOADS[z][c]
+                if share > 0:
+                    dst, src = dealt_views(grouped, w1_raw[z, c], c0, 0, share)
+                    nc.vector.tensor_copy(out=dst, in_=src)
+                if share < width:
+                    dst, src = dealt_views(grouped, w1_raw[z, c], c0, share, width)
+                    nc.scalar.copy(out=dst, in_=src)
+            w1_grouped.append(grouped)
+            w1_scales.append(keep.tile([P, H], U8, name="w1_scales%d" % z, align_bytes=64))
+        by_tile = w1_last[:].rearrange("p j (m t) -> p t m j", t=PACK)
+        nc.scalar.copy(out=w1_grouped[-1][:, 0, (H - W_LAST) // PACK :, :], in_=by_tile[:, 0, :, :])
+        dst, src = dealt_views(w1_grouped[-1], w1_last, H - W_LAST, 0, W_LAST)
+        nc.vector.tensor_copy(out=dst[:, :, :, :, 1:], in_=src[:, :, :, :, 1:])
+
+        early_words = keep.tile([P, EARLY_TILES * P], U32, name="early_words", align_bytes=64)
+        late_words = keep.tile([P, H - EARLY_TILES * P], U32, name="late_words", tag="w1_last", align_bytes=64)
+        closing_words = keep.tile([P, H], U32, name="closing_words", tag="closing_words", align_bytes=64)
 
         def w1_words(z, t0, t1):
-            if z == 1:
-                return words1[:, t0 * P : t1 * P]
-            return head0[:] if t0 == 0 else rest0[:, (t0 - 1) * P : (t1 - 1) * P]
+            if z == PASSES - 1:
+                return closing_words[:, t0 * P : t1 * P]
+            if t0 < EARLY_TILES:
+                return early_words[:, t0 * P : t1 * P]
+            return late_words[:, (t0 - EARLY_TILES) * P : (t1 - EARLY_TILES) * P]
 
-        for t0, t1 in ((0, 1), (1, 2), (2, 4)):
-            for z in range(PASSES):
-                quantize(w1_words(z, t0, t1), w1_scales[z][:, t0 * P : t1 * P], w1_bf[z][:, t0:t1, :, :].rearrange("p t m j -> p (t m j)"))
+        def quantize_w1(z, t0, t1):
+            grouped = w1_grouped[z][:, t0:t1, :, :].rearrange("p t m j -> p (t m j)")
+            quantize(w1_words(z, t0, t1), w1_scales[z][:, t0 * P : t1 * P], grouped)
+
+        quantize_w1(0, 0, EARLY_TILES)
+        for t in range(EARLY_TILES):
+            quantize_w1(1, t, t + 1)
+        for z in range(PASSES):
+            quantize_w1(z, EARLY_TILES, PACK)
 
         h = []
         for t in range(PACK):
-            cols = slice(t * P, (t + 1) * P)
             h_t = keep.tile([P, S], F32, name="h%d" % t)
             width = S // 2 if t == 0 else S
-            accs = [psum.tile([P, width], F32, name="acc%d_%d" % (t, b), tag="acc%d_%d" % (t, b)) for b in range(S // width)]
+            banks = [psum.tile([P, width], F32, name="h_acc%d_%d" % (t, b), tag="bank%d_%d" % (t, b)) for b in range(S // width)]
             for z in range(PASSES):
-                for b, acc in enumerate(accs):
-                    nodes = slice(b * width, (b + 1) * width)
-                    nc.tensor.matmul_mx(
-                        out=acc[:],
-                        lhsT=w1_words(z, t, t + 1).bitcast(FP8X4),
-                        lhsT_scale=w1_scales[z][:, cols],
-                        rhs=picked_words[z][:, nodes].bitcast(FP8X4),
-                        rhs_scale=picked_scales[4 * z :, nodes],
+                for b, bank in enumerate(banks):
+                    entries = slice(b * width, (b + 1) * width)
+                    multiply(
+                        bank[:],
+                        w1_words(z, t, t + 1),
+                        w1_scales[z][:, t * P : (t + 1) * P],
+                        picked_words[z][:, entries],
+                        picked_scales[SCALE_ROWS * z :, entries],
                         start=(z == 0),
                         stop=(z == PASSES - 1),
                     )
-            for b, acc in enumerate(accs):
-                nc.scalar.activation(out=h_t[:, b * width : (b + 1) * width], in_=acc[:], func=RELU)
+            for b, bank in enumerate(banks):
+                nc.scalar.activation(out=h_t[:, b * width : (b + 1) * width], in_=bank[:], func=RELU)
             h.append(h_t)
 
-        first = keep.tile([P, PACK, V], BF16, name="first", tag="planes")
+        def gather(dst, t, entries):
+            nc.vector.tensor_copy(out=dst, in_=h[t][:].indirect(entries))
+
+        cen_halves = [cen_sb[:, half * HALF // LIST_ROWS : (half + 1) * HALF // LIST_ROWS] for half in range(2)]
+        shared = keep.tile([P, PACK * V + HALF], BF16, name="shared")
+        first = shared[:, : PACK * V].rearrange("p (t v) -> p t v", t=PACK)
+        centre0 = shared[:, PACK * V - (PACK - 1) * HALF :].rearrange("p (t v) -> p t v", t=PACK)
         second = keep.tile([P, PACK, V], BF16, name="second")
         for t in range(PACK):
-            nc.vector.tensor_copy(out=first[:, t, :], in_=h[t][:].indirect(pos1_sb[:]))
-            nc.vector.tensor_copy(out=second[:, t, :], in_=h[t][:].indirect(pos2_sb[:]))
+            gather(first[:, t, :], t, pos1_sb[:])
+            gather(second[:, t, :], t, pos2_sb[:])
+        gather(centre0[:, PACK - 1, :], PACK - 1, cen_halves[0])
 
-        w23_bf = keep.tile([P, 2 * N, PACK], BF16, name="w23_bf", tag="w23_bf", align_bytes=64)
-        interleave("scalar", w23_bf[:, :N, :], w3_raw[:])
-        interleave("scalar", w23_bf[:, N:, :], w2_raw[:])
-        w23_words = keep.tile([P, 2 * N], U32, name="w23_words", align_bytes=64)
-        w23_scales = keep.tile([P, 2 * N], U8, name="w23_scales", align_bytes=64)
-        quantize(w23_words[:], w23_scales[:], w23_bf[:].rearrange("p c j -> p (c j)"))
+        w32_grouped = keep.tile([P, 2 * N, PACK], BF16, name="w32_grouped", tag="closing_words", align_bytes=64)
+        interleave("scalar", w32_grouped[:, :N, :], w3_raw[:])
+        interleave("scalar", w32_grouped[:, N:, :], w2_raw[:])
+        w32_words = keep.tile([P, 2 * N], U32, name="w32_words", align_bytes=64)
+        w32_scales = keep.tile([P, 2 * N], U8, name="w32_scales", align_bytes=64)
+        quantize(w32_words[:], w32_scales[:], w32_grouped[:].rearrange("p c j -> p (c j)"))
 
         largest = keep.tile([P, PACK, V], BF16, name="largest")
-        nc.vector.tensor_tensor(out=largest[:], in0=first[:], in1=second[:], op=MAX)
-        z_bf = keep.tile([P, V, PACK], BF16, name="z_bf", tag="w2_raw", align_bytes=64)
-        interleave("scalar", z_bf[:], largest[:])
+        nc.vector.tensor_tensor(out=largest[:], in0=first, in1=second[:], op=MAX)
+        z_grouped = keep.tile([P, V, PACK], BF16, name="z_grouped", tag="w2_raw", align_bytes=64)
+        interleave("scalar", z_grouped[:], largest[:])
         z_words = keep.tile([P, V], U32, name="z_words", align_bytes=64)
         z_scales = keep.tile([P, V], U8, name="z_scales", align_bytes=64)
 
-        centre = []
-        for half in range(2):
-            if half == 0:
-                planes = keep.tile([P, PACK, HALF], BF16, name="centre0", tag="planes")
-            else:
-                planes = keep.tile([P, PACK, HALF], BF16, name="centre1", tag="w23_bf", align_bytes=64)
-            entries = cen_sb[:, half * HALF // 16 : (half + 1) * HALF // 16]
-            for t in range(PACK):
-                nc.vector.tensor_copy(out=planes[:, t, :], in_=h[t][:].indirect(entries))
-            centre.append(planes)
-        quantize(z_words[:], z_scales[:], z_bf[:].rearrange("p c j -> p (c j)"))
+        for t in range(PACK - 1):
+            gather(centre0[:, t, :], t, cen_halves[0])
+        centre0_grouped = keep.tile([P, HALF, PACK], BF16, name="centre0_grouped", align_bytes=64)
+        interleave("scalar", centre0_grouped[:], centre0)
+        centre1 = keep.tile([P, PACK, HALF], BF16, name="centre1", tag="closing_words", align_bytes=64)
+        for t in range(PACK):
+            gather(centre1[:, t, :], t, cen_halves[1])
+        quantize(z_words[:], z_scales[:], z_grouped[:].rearrange("p c j -> p (c j)"))
+        centre1_grouped = keep.tile([P, HALF, PACK], BF16, name="centre1_grouped", tag="w2_raw", align_bytes=64)
+        interleave("vector", centre1_grouped[:], centre1[:])
 
-        for half in range(2):
+        for half, centre_grouped in enumerate((centre0_grouped, centre1_grouped)):
             targets = slice(half * HALF, (half + 1) * HALF)
-            if half == 0:
-                c_bf = keep.tile([P, HALF, PACK], BF16, name="c_bf0", align_bytes=64)
-                interleave("scalar", c_bf[:], centre[half][:])
-            else:
-                c_bf = keep.tile([P, HALF, PACK], BF16, name="c_bf1", tag="w2_raw", align_bytes=64)
-                interleave("vector", c_bf[:], centre[half][:])
-            c_words = keep.tile([P, HALF], U32, name="c_words%d" % half, align_bytes=64)
-            c_scales = keep.tile([P, HALF], U8, name="c_scales%d" % half, align_bytes=64)
-            quantize(c_words[:], c_scales[:], c_bf[:].rearrange("p c j -> p (c j)"))
+            centre_words = keep.tile([P, HALF], U32, name="centre_words%d" % half, align_bytes=64)
+            centre_scales = keep.tile([P, HALF], U8, name="centre_scales%d" % half, align_bytes=64)
+            quantize(centre_words[:], centre_scales[:], centre_grouped[:].rearrange("p c j -> p (c j)"))
 
             staged = keep.tile([P, N // P, HALF], F32, name="staged%d" % half)
             for a in range(N // P):
-                res = psum.tile([P, HALF], F32, name="res%d_%d" % (half, a), tag="acc%d_0" % (2 * half + a))
-                c3 = slice(a * P, (a + 1) * P)
-                c2 = slice(N + a * P, N + (a + 1) * P)
-                nc.tensor.matmul_mx(out=res[:], lhsT=w23_words[:, c3].bitcast(FP8X4), lhsT_scale=w23_scales[:, c3],
-                                    rhs=z_words[:, targets].bitcast(FP8X4), rhs_scale=z_scales[:, targets], start=True, stop=False)
-                nc.tensor.matmul_mx(out=res[:], lhsT=w23_words[:, c2].bitcast(FP8X4), lhsT_scale=w23_scales[:, c2],
-                                    rhs=c_words[:].bitcast(FP8X4), rhs_scale=c_scales[:], start=False, stop=True)
-                if half == 0 or a == 0:
-                    nc.scalar.activation(out=staged[:, a, :], in_=res[:], func=RELU)
+                bank = psum.tile([P, HALF], F32, name="out_acc%d_%d" % (half, a), tag="bank%d_0" % (2 * half + a))
+                of_w3 = slice(a * P, (a + 1) * P)
+                of_w2 = slice(N + a * P, N + (a + 1) * P)
+                multiply(bank[:], w32_words[:, of_w3], w32_scales[:, of_w3], z_words[:, targets], z_scales[:, targets], True, False)
+                multiply(bank[:], w32_words[:, of_w2], w32_scales[:, of_w2], centre_words[:], centre_scales[:], False, True)
+                if (half, a) == (1, 1):
+                    nc.vector.tensor_scalar(out=staged[:, a, :], in0=bank[:], scalar1=0.0, scalar2=None, op0=MAX)
                 else:
-                    nc.vector.tensor_scalar(out=staged[:, a, :], in0=res[:], scalar1=0.0, scalar2=None, op0=MAX)
+                    nc.scalar.activation(out=staged[:, a, :], in_=bank[:], func=RELU)
             nc.sync.dma_start(out=out[:, targets].rearrange("(a p) v -> p a v", p=P), in_=staged[:])

@@ -40,10 +40,13 @@ def tile_picked_sagecat_maxrelu_e_kernel(tc, xT, w1, w2, w3, offs, cen, pos1, po
             nc.sync.dma_start(tile[:], src)
             return tile
 
+        def load_into(raw, src, z, c0, width):
+            rows = src[z * K_PASS : (z + 1) * K_PASS, c0 : c0 + width]
+            nc.sync.dma_start(out=raw, in_=rows.rearrange("(p j) w -> p j w", j=PACK))
+
         def load_rows(src, z, c0, width, name):
             raw = keep.tile([P, PACK, width], F32, name=name, tag=name, align_bytes=64)
-            rows = src[z * K_PASS : (z + 1) * K_PASS, c0 : c0 + width]
-            nc.sync.dma_start(out=raw[:], in_=rows.rearrange("(p j) w -> p j w", j=PACK))
+            load_into(raw[:], src, z, c0, width)
             return raw
 
         def interleave(engine, grouped, planes):
@@ -86,7 +89,9 @@ def tile_picked_sagecat_maxrelu_e_kernel(tc, xT, w1, w2, w3, offs, cen, pos1, po
         pos2_sb = load_list(pos2, "pos2_sb")
         cen_sb = load_list(cen, "cen_sb")
         w3_raw = load_rows(w3, 0, 0, N, "w3_raw")
-        w2_raw = load_rows(w2, 0, 0, N, "w2_raw")
+        w2_room = keep.tile([P, PACK * N + HALF // 2], F32, name="w2_room")
+        w2_raw = w2_room[:, : PACK * N].rearrange("p (j w) -> p j w", j=PACK)
+        load_into(w2_raw, w2, 0, 0, N)
 
         x_scales = keep.tile([P, T], U8, name="x_scales", align_bytes=64)
         nc.gpsimd.memset(x_scales[:], 0)
@@ -178,9 +183,10 @@ def tile_picked_sagecat_maxrelu_e_kernel(tc, xT, w1, w2, w3, offs, cen, pos1, po
             nc.vector.tensor_copy(out=dst, in_=h[t][:].indirect(entries))
 
         cen_halves = [cen_sb[:, half * HALF // LIST_ROWS : (half + 1) * HALF // LIST_ROWS] for half in range(2)]
-        shared = keep.tile([P, PACK * V + HALF], BF16, name="shared")
-        first = shared[:, : PACK * V].rearrange("p (t v) -> p t v", t=PACK)
-        centre0 = shared[:, PACK * V - (PACK - 1) * HALF :].rearrange("p (t v) -> p t v", t=PACK)
+        room = w2_room[:].bitcast(BF16)
+        centre0 = room[:, 2 * PACK * N - (PACK - 1) * HALF :].rearrange("p (t v) -> p t v", t=PACK)
+        centre1 = room[:, : PACK * HALF].rearrange("p (t v) -> p t v", t=PACK)
+        first = keep.tile([P, PACK, V], BF16, name="first")
         second = keep.tile([P, PACK, V], BF16, name="second")
         for t in range(PACK):
             gather(first[:, t, :], t, pos1_sb[:])
@@ -189,14 +195,14 @@ def tile_picked_sagecat_maxrelu_e_kernel(tc, xT, w1, w2, w3, offs, cen, pos1, po
 
         w32_grouped = keep.tile([P, 2 * N, PACK], BF16, name="w32_grouped", tag="closing_words", align_bytes=64)
         interleave("scalar", w32_grouped[:, :N, :], w3_raw[:])
-        interleave("scalar", w32_grouped[:, N:, :], w2_raw[:])
+        interleave("scalar", w32_grouped[:, N:, :], w2_raw)
         w32_words = keep.tile([P, 2 * N], U32, name="w32_words", align_bytes=64)
         w32_scales = keep.tile([P, 2 * N], U8, name="w32_scales", align_bytes=64)
         quantize(w32_words[:], w32_scales[:], w32_grouped[:].rearrange("p c j -> p (c j)"))
 
         largest = keep.tile([P, PACK, V], BF16, name="largest")
-        nc.vector.tensor_tensor(out=largest[:], in0=first, in1=second[:], op=MAX)
-        z_grouped = keep.tile([P, V, PACK], BF16, name="z_grouped", tag="w2_raw", align_bytes=64)
+        nc.vector.tensor_tensor(out=largest[:], in0=first[:], in1=second[:], op=MAX)
+        z_grouped = keep.tile([P, V, PACK], BF16, name="z_grouped", align_bytes=64)
         interleave("scalar", z_grouped[:], largest[:])
         z_words = keep.tile([P, V], U32, name="z_words", align_bytes=64)
         z_scales = keep.tile([P, V], U8, name="z_scales", align_bytes=64)
@@ -205,12 +211,11 @@ def tile_picked_sagecat_maxrelu_e_kernel(tc, xT, w1, w2, w3, offs, cen, pos1, po
             gather(centre0[:, t, :], t, cen_halves[0])
         centre0_grouped = keep.tile([P, HALF, PACK], BF16, name="centre0_grouped", align_bytes=64)
         interleave("scalar", centre0_grouped[:], centre0)
-        centre1 = keep.tile([P, PACK, HALF], BF16, name="centre1", tag="closing_words", align_bytes=64)
         for t in range(PACK):
             gather(centre1[:, t, :], t, cen_halves[1])
         quantize(z_words[:], z_scales[:], z_grouped[:].rearrange("p c j -> p (c j)"))
-        centre1_grouped = keep.tile([P, HALF, PACK], BF16, name="centre1_grouped", tag="w2_raw", align_bytes=64)
-        interleave("vector", centre1_grouped[:], centre1[:])
+        centre1_grouped = keep.tile([P, HALF, PACK], BF16, name="centre1_grouped", align_bytes=64)
+        interleave("vector", centre1_grouped[:], centre1)
 
         for half, centre_grouped in enumerate((centre0_grouped, centre1_grouped)):
             targets = slice(half * HALF, (half + 1) * HALF)

from contextlib import ExitStack

import concourse.mybir as mybir

K, T, S, V, H, N = 1024, 1024, 512, 256, 512, 256
FLOPS = 2 * K * H * S + 2 * 2 * H * N * V

F32 = mybir.dt.float32
BF16 = mybir.dt.bfloat16
U32 = mybir.dt.uint32
U16 = mybir.dt.uint16
U8 = mybir.dt.uint8
FP8X4 = mybir.dt.float8_e4m3fn_x4
COPY = mybir.ActivationFunctionType.Copy
RELU = mybir.ActivationFunctionType.Relu
MAX = mybir.AluOpType.max

P = 128
PACK = 4
K_PASS = P * PACK
PASSES = K // K_PASS
SCALE_ROWS = 4
LIST_ROWS = 16
HALF = V // 2

X_LOADS = (((512, 256), (512, 320)), ((256, 0), (256, 0), (256, 128), (128, 0), (128, 128)))
W_LOADS = (((256, 0), (256, 0)), ((256, 128), (128, 128)))
W_LAST = 128
EARLY_TILES = 2


def tile_picked_sagecat_maxrelu_e_kernel(tc, xT, w1, w2, w3, offs, cen, pos1, pos2, out):
    nc = tc.nc
    with ExitStack() as ctx:
        keep = ctx.enter_context(tc.tile_pool(name="keep", bufs=1))
        psum = ctx.enter_context(tc.psum_pool(name="psum", bufs=1))

        def load_list(src, name):
            tile = keep.tile(list(src.shape), U16, name=name)
            nc.sync.dma_start(tile[:], src)
            return tile

        def load_into(raw, src, z, c0, width):
            rows = src[z * K_PASS : (z + 1) * K_PASS, c0 : c0 + width]
            nc.sync.dma_start(out=raw, in_=rows.rearrange("(p j) w -> p j w", j=PACK))

        def load_rows(src, z, c0, width, name):
            raw = keep.tile([P, PACK, width], F32, name=name, tag=name, align_bytes=64)
            load_into(raw[:], src, z, c0, width)
            return raw

        def interleave(engine, grouped, planes):
            dst = grouped.rearrange("p (c i) j -> p c j i", i=4)
            src = planes.rearrange("p j (c i) -> p c j i", i=4)
            if engine == "vector":
                nc.vector.tensor_copy(out=dst, in_=src)
            else:
                nc.scalar.activation(out=dst, in_=src, func=COPY)

        def quantize(words, scales, grouped):
            nc.vector.quantize_mx(out=words.bitcast(FP8X4), scales=scales, in_=grouped)

        def multiply(acc, lhs_words, lhs_scales, rhs_words, rhs_scales, start, stop):
            nc.tensor.matmul_mx(
                out=acc,
                lhsT=lhs_words.bitcast(FP8X4),
                lhsT_scale=lhs_scales,
                rhs=rhs_words.bitcast(FP8X4),
                rhs_scale=rhs_scales,
                start=start,
                stop=stop,
            )

        def starts(loads):
            return [sum(width for width, share in loads[:c]) for c in range(len(loads))]

        x_raw = {}
        for z in range(PASSES):
            for c, c0 in enumerate(starts(X_LOADS[z])):
                x_raw[z, c] = load_rows(xT, z, c0, X_LOADS[z][c][0], "x_raw%d_%d" % (z, c))
                if (z, c) == (0, 0):
                    offs_sb = load_list(offs, "offs_sb")
        w1_raw = {}
        for z in range(PASSES):
            for c, c0 in enumerate(starts(W_LOADS[z])):
                w1_raw[z, c] = load_rows(w1, z, c0, W_LOADS[z][c][0], "w1_raw%d_%d" % (z, c))
        w1_last = load_rows(w1, PASSES - 1, H - W_LAST, W_LAST, "w1_last")
        pos1_sb = load_list(pos1, "pos1_sb")
        pos2_sb = load_list(pos2, "pos2_sb")
        cen_sb = load_list(cen, "cen_sb")
        w3_raw = load_rows(w3, 0, 0, N, "w3_raw")
        w2_room = keep.tile([P, PACK * N + HALF // 2], F32, name="w2_room")
        w2_raw = w2_room[:, : PACK * N].rearrange("p (j w) -> p j w", j=PACK)
        load_into(w2_raw, w2, 0, 0, N)

        x_scales = keep.tile([P, T], U8, name="x_scales", align_bytes=64)
        nc.gpsimd.memset(x_scales[:], 0)
        picked_words = []
        for z in range(PASSES):
            x_words = keep.tile([P, T], U32, name="x_words%d" % z, align_bytes=64)
            for c, c0 in enumerate(starts(X_LOADS[z])):
                width, share = X_LOADS[z][c]
                x_grouped = keep.tile([P, width, PACK], BF16, name="x_grouped%d_%d" % (z, c), align_bytes=64)
                if share > 0:
                    interleave("vector", x_grouped[:, :share, :], x_raw[z, c][:, :, :share])
                if share < width:
                    interleave("scalar", x_grouped[:, share:, :], x_raw[z, c][:, :, share:])
                nodes = slice(c0, c0 + width)
                quantize(x_words[:, nodes], x_scales[SCALE_ROWS * z :, nodes], x_grouped[:].rearrange("p c j -> p (c j)"))
            picked = keep.tile([P, S], U32, name="picked_words%d" % z, align_bytes=64)
            nc.vector.tensor_copy(out=picked[:], in_=x_words[:].indirect(offs_sb[:]))
            picked_words.append(picked)
        picked_scales = keep.tile([P, S], U8, name="picked_scales", align_bytes=64)
        nc.vector.tensor_copy(out=picked_scales[:], in_=x_scales[:].indirect(offs_sb[:]))

        def dealt_views(grouped, raw, c0, lo, hi):
            places = slice((c0 + lo) // PACK, (c0 + hi) // PACK)
            dst = grouped[:, :, places, :].rearrange("p t (a b) j -> p a j b t", b=2)
            src = raw[:, :, lo:hi].rearrange("p j (a b t) -> p a j b t", b=2, t=PACK)
            return dst, src

        w1_grouped, w1_scales = [], []
        for z in range(PASSES):
            grouped = keep.tile([P, PACK, P, PACK], BF16, name="w1_grouped%d" % z, align_bytes=64)
            for c, c0 in enumerate(starts(W_LOADS[z])):
                width, share = W_LOADS[z][c]
                if share > 0:
                    dst, src = dealt_views(grouped, w1_raw[z, c], c0, 0, share)
                    nc.vector.tensor_copy(out=dst, in_=src)
                if share < width:
                    dst, src = dealt_views(grouped, w1_raw[z, c], c0, share, width)
                    nc.scalar.copy(out=dst, in_=src)
            w1_grouped.append(grouped)
            w1_scales.append(keep.tile([P, H], U8, name="w1_scales%d" % z, align_bytes=64))
        by_tile = w1_last[:].rearrange("p j (m t) -> p t m j", t=PACK)
        nc.scalar.copy(out=w1_grouped[-1][:, 0, (H - W_LAST) // PACK :, :], in_=by_tile[:, 0, :, :])
        dst, src = dealt_views(w1_grouped[-1], w1_last, H - W_LAST, 0, W_LAST)
        nc.vector.tensor_copy(out=dst[:, :, :, :, 1:], in_=src[:, :, :, :, 1:])

        early_words = keep.tile([P, EARLY_TILES * P], U32, name="early_words", align_bytes=64)
        late_words = keep.tile([P, H - EARLY_TILES * P], U32, name="late_words", tag="w1_last", align_bytes=64)
        closing_words = keep.tile([P, H], U32, name="closing_words", tag="closing_words", align_bytes=64)

        def w1_words(z, t0, t1):
            if z == PASSES - 1:
                return closing_words[:, t0 * P : t1 * P]
            if t0 < EARLY_TILES:
                return early_words[:, t0 * P : t1 * P]
            return late_words[:, (t0 - EARLY_TILES) * P : (t1 - EARLY_TILES) * P]

        def quantize_w1(z, t0, t1):
            grouped = w1_grouped[z][:, t0:t1, :, :].rearrange("p t m j -> p (t m j)")
            quantize(w1_words(z, t0, t1), w1_scales[z][:, t0 * P : t1 * P], grouped)

        quantize_w1(0, 0, EARLY_TILES)
        for t in range(EARLY_TILES):
            quantize_w1(1, t, t + 1)
        for z in range(PASSES):
            quantize_w1(z, EARLY_TILES, PACK)

        h = []
        for t in range(PACK):
            h_t = keep.tile([P, S], F32, name="h%d" % t)
            width = S // 2 if t == 0 else S
            banks = [psum.tile([P, width], F32, name="h_acc%d_%d" % (t, b), tag="bank%d_%d" % (t, b)) for b in range(S // width)]
            for z in range(PASSES):
                for b, bank in enumerate(banks):
                    entries = slice(b * width, (b + 1) * width)
                    multiply(
                        bank[:],
                        w1_words(z, t, t + 1),
                        w1_scales[z][:, t * P : (t + 1) * P],
                        picked_words[z][:, entries],
                        picked_scales[SCALE_ROWS * z :, entries],
                        start=(z == 0),
                        stop=(z == PASSES - 1),
                    )
            for b, bank in enumerate(banks):
                nc.scalar.activation(out=h_t[:, b * width : (b + 1) * width], in_=bank[:], func=RELU)
            h.append(h_t)

        def gather(dst, t, entries):
            nc.vector.tensor_copy(out=dst, in_=h[t][:].indirect(entries))

        cen_halves = [cen_sb[:, half * HALF // LIST_ROWS : (half + 1) * HALF // LIST_ROWS] for half in range(2)]
        room = w2_room[:].bitcast(BF16)
        centre0 = room[:, 2 * PACK * N - (PACK - 1) * HALF :].rearrange("p (t v) -> p t v", t=PACK)
        centre1 = room[:, : PACK * HALF].rearrange("p (t v) -> p t v", t=PACK)
        first = keep.tile([P, PACK, V], BF16, name="first")
        second = keep.tile([P, PACK, V], BF16, name="second")
        for t in range(PACK):
            gather(first[:, t, :], t, pos1_sb[:])
            gather(second[:, t, :], t, pos2_sb[:])
        gather(centre0[:, PACK - 1, :], PACK - 1, cen_halves[0])

        w32_grouped = keep.tile([P, 2 * N, PACK], BF16, name="w32_grouped", tag="closing_words", align_bytes=64)
        interleave("scalar", w32_grouped[:, :N, :], w3_raw[:])
        interleave("scalar", w32_grouped[:, N:, :], w2_raw)
        w32_words = keep.tile([P, 2 * N], U32, name="w32_words", align_bytes=64)
        w32_scales = keep.tile([P, 2 * N], U8, name="w32_scales", align_bytes=64)
        quantize(w32_words[:], w32_scales[:], w32_grouped[:].rearrange("p c j -> p (c j)"))

        largest = keep.tile([P, PACK, V], BF16, name="largest")
        nc.vector.tensor_tensor(out=largest[:], in0=first[:], in1=second[:], op=MAX)
        z_grouped = keep.tile([P, V, PACK], BF16, name="z_grouped", align_bytes=64)
        interleave("scalar", z_grouped[:], largest[:])
        z_words = keep.tile([P, V], U32, name="z_words", align_bytes=64)
        z_scales = keep.tile([P, V], U8, name="z_scales", align_bytes=64)

        for t in range(PACK - 1):
            gather(centre0[:, t, :], t, cen_halves[0])
        centre0_grouped = keep.tile([P, HALF, PACK], BF16, name="centre0_grouped", align_bytes=64)
        interleave("scalar", centre0_grouped[:], centre0)
        for t in range(PACK):
            gather(centre1[:, t, :], t, cen_halves[1])
        quantize(z_words[:], z_scales[:], z_grouped[:].rearrange("p c j -> p (c j)"))
        centre1_grouped = keep.tile([P, HALF, PACK], BF16, name="centre1_grouped", align_bytes=64)
        interleave("vector", centre1_grouped[:], centre1)

        for half, centre_grouped in enumerate((centre0_grouped, centre1_grouped)):
            targets = slice(half * HALF, (half + 1) * HALF)
            centre_words = keep.tile([P, HALF], U32, name="centre_words%d" % half, align_bytes=64)
            centre_scales = keep.tile([P, HALF], U8, name="centre_scales%d" % half, align_bytes=64)
            quantize(centre_words[:], centre_scales[:], centre_grouped[:].rearrange("p c j -> p (c j)"))

            staged = keep.tile([P, N // P, HALF], F32, name="staged%d" % half)
            for a in range(N // P):
                bank = psum.tile([P, HALF], F32, name="out_acc%d_%d" % (half, a), tag="bank%d_0" % (2 * half + a))
                of_w3 = slice(a * P, (a + 1) * P)
                of_w2 = slice(N + a * P, N + (a + 1) * P)
                multiply(bank[:], w32_words[:, of_w3], w32_scales[:, of_w3], z_words[:, targets], z_scales[:, targets], True, False)
                multiply(bank[:], w32_words[:, of_w2], w32_scales[:, of_w2], centre_words[:], centre_scales[:], False, True)
                if (half, a) == (1, 1):
                    nc.vector.tensor_scalar(out=staged[:, a, :], in0=bank[:], scalar1=0.0, scalar2=None, op0=MAX)
                else:
                    nc.scalar.activation(out=staged[:, a, :], in_=bank[:], func=RELU)
            nc.sync.dma_start(out=out[:, targets].rearrange("(a p) v -> p a v", p=P), in_=staged[:])
